import numpy as np
import ml_dtypes


def mxq(x, axis, fmt="e4m3"):
    dtype, down = {"e4m3": (ml_dtypes.float8_e4m3fn, 7), "e5m2": (ml_dtypes.float8_e5m2, 14)}[fmt]
    v = np.moveaxis(np.asarray(x, np.float32).astype(ml_dtypes.bfloat16).astype(np.float64), axis, -1)
    blocks = v.reshape(v.shape[:-1] + (-1, 32))
    amax = np.abs(blocks).max(-1, keepdims=True)
    byte = np.maximum(np.where(amax > 0, np.frexp(amax)[1] - 1 + 127, 0) - down, 1)
    scale = np.exp2(byte - 127.0)
    codes = (blocks / scale).astype(np.float32).astype(dtype).astype(np.float64)
    return np.moveaxis((codes * scale).reshape(v.shape), -1, axis)


WIDE = False


def mx_kscale(k):
    if not WIDE:
        return np.ones(k)
    levels = np.array([10, -10, 5, -5, 0])
    if k % 512:
        return np.exp2(np.random.permutation(np.resize(levels, k // 32))).repeat(32)
    a = np.empty((k // 512, 16))
    for p in range(k // 512):
        a[p, :8] = np.random.permutation(np.resize(levels, 8))
        for g in range(8):
            far = levels[np.abs(levels - a[p, g]) >= 10]
            a[p, g + 8] = far[np.random.randint(len(far))]
    return np.exp2(a.ravel()).repeat(32)


def f64(x):
    return np.asarray(x).astype(np.float64)


E2M1 = np.array([0.0, 0.5, 1.0, 1.5, 2.0, 3.0, 4.0, 6.0, -0.0, -0.5, -1.0, -1.5, -2.0, -3.0, -4.0, -6.0])


def pack_weight(w, fmt):
    k, n = w.shape
    w = f64(np.asarray(w, np.float32).astype(ml_dtypes.bfloat16)).reshape(k // 32, 32, n)
    amax = np.abs(w).max(1)
    if fmt == "e4m3":
        byte = np.frexp(amax)[1] - 1 + 127 - 7
    else:
        mant, ex = np.frexp(amax / 6.0)
        byte = np.where(mant > 0.5, ex, ex - 1) + 127
    byte = np.clip(np.where(amax > 0, byte, 1), 1, 254)
    scaled = (w * np.exp2(127.0 - byte)[:, None, :]).reshape(k, n).astype(np.float32)
    by_word = np.ascontiguousarray(scaled.reshape(k // 512, 128, 4, n).transpose(0, 1, 3, 2))
    if fmt == "e4m3":
        words = by_word.astype(ml_dtypes.float8_e4m3fn).view(np.uint8)
    else:
        c = by_word.astype(ml_dtypes.float4_e2m1fn).view(np.uint8) & 0xF
        words = (c[..., 0::2] | (c[..., 1::2] << 4)).reshape(k // 512, 128, 2 * n)
    return np.ascontiguousarray(words), np.ascontiguousarray(byte.astype(np.uint8).reshape(k // 512, 16, n))


def unpack_weight(words, scales, fmt):
    g, _, n = scales.shape
    words = np.ascontiguousarray(words).reshape(g, 128, n, -1)
    if fmt == "e4m3":
        vals = words.view(ml_dtypes.float8_e4m3fn).astype(np.float64)
    else:
        nib = np.empty((g, 128, n, 4), np.uint8)
        nib[..., 0::2] = words & 0xF
        nib[..., 1::2] = words >> 4
        vals = E2M1[nib]
    vals = vals * np.repeat(np.exp2(scales.astype(np.float64) - 127.0), 8, axis=1)[..., None]
    return vals.transpose(0, 1, 3, 2).reshape(g * 512, n)


D, K, M, T = 128, 1024, 512, 1536


def setup_inputs():
    n = np.random.standard_normal
    s = mx_kscale(K)[:, None]
    p_w0 = pack_weight(n((K, M)) / np.sqrt(K) / s, "e2m1")
    p_w1 = pack_weight(n((K, M)) / np.sqrt(K) / s, "e4m3")
    return {
        "x": (n((K, T + 2 * D)) * s).astype(np.float32),
        "w0_words": p_w0[0],
        "w0_scales": p_w0[1],
        "w1_words": p_w1[0],
        "w1_scales": p_w1[1],
        "w2": (n((K, M)) / np.sqrt(K) / s).astype(np.float32),
    }


def reference(x, w0_words, w0_scales, w1_words, w1_scales, w2):
    x_ = mxq(f64(x), 0, "e4m3")
    w0_ = unpack_weight(w0_words, w0_scales, "e2m1")
    w1_ = unpack_weight(w1_words, w1_scales, "e4m3")
    w2_ = mxq(f64(w2), 0, "e4m3")
    y = w0_.T @ x_[:, :T] + w1_.T @ x_[:, D:D + T] + w2_.T @ x_[:, 2 * D:]
    return y

@@ -1,0 +1,204 @@
+from contextlib import ExitStack
+
+import concourse.mybir as mybir
+
+D, K, M, T = 128, 1024, 512, 1536
+FLOPS = 2 * 3 * K * M * T
+
+F32 = mybir.dt.float32
+BF16 = mybir.dt.bfloat16
+I32 = mybir.dt.int32
+U32 = mybir.dt.uint32
+U8 = mybir.dt.uint8
+FP8X4 = mybir.dt.float8_e4m3fn_x4
+FP4X4 = mybir.dt.float4_e2m1fn_x4
+
+P = 128
+PACK = 4
+K_PASS = P * PACK
+PASSES = K // K_PASS
+BANK = 512
+M_TILES = M // P
+TAPS = 3
+X_COLS = T + 2 * D
+X_EDGES = (0, 640, 1152, 1536, X_COLS)
+LEAD = 128
+ALIGN = 256
+
+
+def tile_mix_dconv_fm_none_kernel(tc, x, w0_words, w0_scales, w1_words, w1_scales, w2, out):
+    nc = tc.nc
+    with ExitStack() as ctx:
+        sb = ctx.enter_context(tc.tile_pool(name="sb", bufs=1))
+        psum = ctx.enter_context(tc.psum_pool(name="psum", bufs=1))
+        ctx.enter_context(tc.manual_schedule())
+
+        x_codes = [sb.tile([P, X_COLS], U32, name=f"x_codes{a}", align_bytes=ALIGN) for a in range(PASSES)]
+        x_scales = [sb.tile([P, X_COLS], U8, name=f"x_scales{a}", align_bytes=ALIGN) for a in range(PASSES)]
+        w2_codes = [sb.tile([P, M], U32, name=f"w2_codes{a}", align_bytes=ALIGN) for a in range(PASSES)]
+        w2_planes = [sb.tile([P, M], U8, name=f"w2_scales{a}", align_bytes=ALIGN) for a in range(PASSES)]
+        w0_codes = sb.tile([P, PASSES * 2 * M], U8, name="w0_codes", align_bytes=ALIGN)
+        w1_codes = sb.tile([P, PASSES * 4 * M], U8, name="w1_codes", align_bytes=ALIGN)
+        w0_plane = sb.tile([P, PASSES * M], U8, name="w0_plane", align_bytes=ALIGN)
+        w1_plane = sb.tile([P, PASSES * M], U8, name="w1_plane", align_bytes=ALIGN)
+        banks = [psum.tile([P, BANK], F32, name=f"bank{b}") for b in range(2 * M_TILES)]
+
+        def load_rows(name, src, a, lo, hi):
+            raw = sb.tile([P, PACK, hi - lo], F32, name=name)
+            rows = src[a * K_PASS : (a + 1) * K_PASS, lo:hi]
+            nc.sync.dma_start(out=raw[:], in_=rows.rearrange("(p j) w -> p j w", j=PACK))
+            return raw
+
+        def load_scales(plane, scales):
+            for q in range(4):
+                nc.sync.dma_start(
+                    out=plane[32 * q : 32 * q + 4, :].bitcast(I32).rearrange("r (a n) -> r a n", a=PASSES),
+                    in_=scales[:, 4 * q : 4 * q + 4, :].bitcast(I32).rearrange("a r n -> r a n"),
+                )
+
+        def load_words(codes, words):
+            nc.sync.dma_start(
+                out=codes[:].bitcast(I32).rearrange("p (a n) -> p a n", a=PASSES),
+                in_=words.bitcast(I32).rearrange("a p n -> p a n"),
+            )
+
+        def interleave(name, raw, lo, hi, on_scalar):
+            grouped = sb.tile([P, PACK * (hi - lo)], BF16, name=name, align_bytes=ALIGN)
+            dst = grouped[:].rearrange("p (c i t) -> p c t i", i=4, t=PACK)
+            src = raw[:, :, lo:hi].rearrange("p t (c i) -> p c t i", i=4)
+            if on_scalar:
+                nc.scalar.copy(out=dst, in_=src)
+            else:
+                nc.vector.tensor_copy(out=dst, in_=src)
+            return grouped
+
+        def quantise(grouped, codes, plane, col):
+            width = grouped.shape[1] // PACK
+            done = 0
+            while done < width:
+                step = max(s for s in (128, 256, 512) if s <= width - done)
+                cols = slice(col + done, col + done + step)
+                nc.vector.quantize_mx(
+                    out=codes[:, cols].bitcast(FP8X4),
+                    scales=plane[:, cols],
+                    in_=grouped[:, PACK * done : PACK * (done + step)],
+                )
+                done = done + step
+
+        def prepare(name, raw, codes, plane, col, lead_on_scalar):
+            width = raw.shape[2]
+            lead = interleave(name + "_lead", raw, 0, LEAD, lead_on_scalar)
+            rest = interleave(name + "_rest", raw, LEAD, width, False)
+            quantise(lead, codes, plane, col)
+            quantise(rest, codes, plane, col + LEAD)
+
+        def weight(tap, a, m):
+            cols = slice(a * M + m * P, a * M + (m + 1) * P)
+            if tap == 0:
+                return w0_codes[:, 2 * cols.start : 2 * cols.stop].bitcast(FP4X4), w0_plane[:, cols]
+            if tap == 1:
+                return w1_codes[:, 4 * cols.start : 4 * cols.stop].bitcast(FP8X4), w1_plane[:, cols]
+            return w2_codes[a][:, m * P : (m + 1) * P].bitcast(FP8X4), w2_planes[a][:, m * P : (m + 1) * P]
+
+        summed = {}
+
+        def bank_of(m, j):
+            return banks[(j % 2) * M_TILES + m]
+
+        def multiply(m, j, tap, a, lo=0, hi=BANK):
+            before = summed.get((m, j), 0)
+            summed[(m, j)] = before + hi - lo
+            codes, plane = weight(tap, a, m)
+            cols = slice(j * BANK + tap * D + lo, j * BANK + tap * D + hi)
+            nc.tensor.matmul_mx(
+                out=bank_of(m, j)[:, lo:hi],
+                lhsT=codes,
+                lhsT_scale=plane,
+                rhs=x_codes[a][:, cols].bitcast(FP8X4),
+                rhs_scale=x_scales[a][:, cols],
+                start=(before == 0),
+                stop=(summed[(m, j)] == TAPS * PASSES * BANK),
+            )
+
+        def finish(m, j, on_scalar):
+            result = sb.tile([P, BANK], F32, name=f"result{m}_{j}")
+            if on_scalar:
+                nc.scalar.copy(out=result[:], in_=bank_of(m, j)[:])
+            else:
+                nc.vector.tensor_copy(out=result[:], in_=bank_of(m, j)[:])
+            nc.sync.dma_start(out=out[m * P : (m + 1) * P, j * BANK : (j + 1) * BANK], in_=result[:])
+
+        nc.vector.memset(w1_plane[:].bitcast(I32), 0)
+        nc.vector.memset(w0_plane[:].bitcast(I32), 0)
+
+        def load_x(c, a):
+            return load_rows(f"x_raw{c}_{a}", x, a, X_EDGES[c], X_EDGES[c + 1])
+
+        x_raw = {(0, 0): load_x(0, 0)}
+        load_scales(w1_plane, w1_scales)
+        load_words(w1_codes, w1_words.rearrange("a p n i -> a p (n i)"))
+        load_scales(w0_plane, w0_scales)
+        load_words(w0_codes, w0_words)
+        x_raw[(0, 1)] = load_x(0, 1)
+        for a in range(PASSES):
+            x_raw[(1, a)] = load_x(1, a)
+        w2_raw = [load_rows(f"w2_raw{a}", w2, a, 0, M) for a in range(PASSES)]
+        for c in (2, 3):
+            for a in range(PASSES):
+                x_raw[(c, a)] = load_x(c, a)
+
+        def prepare_x(c, a, lead_on_scalar):
+            prepare(f"x_bf{c}_{a}", x_raw[(c, a)], x_codes[a], x_scales[a], X_EDGES[c], lead_on_scalar)
+
+        ms = range(M_TILES)
+        for j in (0, 1):
+            for a in range(PASSES):
+                prepare_x(j, a, True)
+                for tap in (1, 0):
+                    for m in ms:
+                        multiply(m, j, tap, a)
+
+        for a in range(PASSES):
+            prepare(f"w2_bf{a}", w2_raw[a], w2_codes[a], w2_planes[a], 0, True)
+            for m in ms:
+                multiply(m, 0, 2, a)
+            for m in ms:
+                multiply(m, 1, 2, a, 0, 256)
+                multiply(m, 1, 2, a, 256, 384)
+
+        def body(m, a):
+            multiply(m, 2, 0, a)
+            multiply(m, 2, 1, a, 0, 256)
+            multiply(m, 2, 1, a, 256, 384)
+            multiply(m, 2, 2, a, 0, 256)
+
+        def edge(m):
+            for a in range(PASSES):
+                multiply(m, 2, 1, a, 384, 512)
+                multiply(m, 2, 2, a, 256, 512)
+
+        finish(0, 0, True)
+        prepare_x(2, 0, True)
+        for m in ms[1:]:
+            finish(m, 0, True)
+        for m in ms:
+            multiply(m, 1, 2, 0, 384, 512)
+        for m in ms:
+            body(m, 0)
+        prepare_x(2, 1, True)
+        for m in ms:
+            multiply(m, 1, 2, 1, 384, 512)
+        for a in range(PASSES):
+            prepare_x(3, a, False)
+        for m in ms:
+            finish(m, 1, True)
+        body(0, 1)
+        body(1, 1)
+        edge(0)
+        finish(0, 2, False)
+        edge(1)
+        finish(1, 2, True)
+        for m in (2, 3):
+            body(m, 1)
+            edge(m)
+            finish(m, 2, m == 3)

@@ -21,7 +21,7 @@ BANK = 512
 M_TILES = M // P
 TAPS = 3
 X_COLS = T + 2 * D
-X_EDGES = (0, 640, 1152, 1536, X_COLS)
+X_EDGES = (0, 384, 640, 1152, 1536, X_COLS)
 LEAD = 128
 ALIGN = 256
 
@@ -56,11 +56,9 @@ def tile_mix_dconv_fm_none_kernel(tc, x, w0_words, w0_scales, w1_words, w1_scale
                     in_=scales[:, 4 * q : 4 * q + 4, :].bitcast(I32).rearrange("a r n -> r a n"),
                 )
 
-        def load_words(codes, words):
-            nc.sync.dma_start(
-                out=codes[:].bitcast(I32).rearrange("p (a n) -> p a n", a=PASSES),
-                in_=words.bitcast(I32).rearrange("a p n -> p a n"),
-            )
+        def load_words(codes, words, a):
+            width = words.shape[2]
+            nc.sync.dma_start(out=codes[:, a * width : (a + 1) * width].bitcast(I32), in_=words[a].bitcast(I32))
 
         def interleave(name, raw, lo, hi, on_scalar):
             grouped = sb.tile([P, PACK * (hi - lo)], BF16, name=name, align_bytes=ALIGN)
@@ -73,24 +71,19 @@ def tile_mix_dconv_fm_none_kernel(tc, x, w0_words, w0_scales, w1_words, w1_scale
             return grouped
 
         def quantise(grouped, codes, plane, col):
-            width = grouped.shape[1] // PACK
-            done = 0
-            while done < width:
-                step = max(s for s in (128, 256, 512) if s <= width - done)
-                cols = slice(col + done, col + done + step)
-                nc.vector.quantize_mx(
-                    out=codes[:, cols].bitcast(FP8X4),
-                    scales=plane[:, cols],
-                    in_=grouped[:, PACK * done : PACK * (done + step)],
-                )
-                done = done + step
+            cols = slice(col, col + grouped.shape[1] // PACK)
+            nc.vector.quantize_mx(out=codes[:, cols].bitcast(FP8X4), scales=plane[:, cols], in_=grouped[:])
 
-        def prepare(name, raw, codes, plane, col, lead_on_scalar):
+        def prepare(name, raw, codes, plane, col, scalar_helps):
             width = raw.shape[2]
-            lead = interleave(name + "_lead", raw, 0, LEAD, lead_on_scalar)
-            rest = interleave(name + "_rest", raw, LEAD, width, False)
+            middle = min(width, LEAD + 256)
+            lead = interleave(name + "_lead", raw, 0, LEAD, scalar_helps)
+            rest = interleave(name + "_rest", raw, LEAD, middle, False)
             quantise(lead, codes, plane, col)
             quantise(rest, codes, plane, col + LEAD)
+            if middle < width:
+                tail = interleave(name + "_tail", raw, middle, width, scalar_helps)
+                quantise(tail, codes, plane, col + middle)
 
         def weight(tap, a, m):
             cols = slice(a * M + m * P, a * M + (m + 1) * P)
@@ -120,13 +113,25 @@ def tile_mix_dconv_fm_none_kernel(tc, x, w0_words, w0_scales, w1_words, w1_scale
                 stop=(summed[(m, j)] == TAPS * PASSES * BANK),
             )
 
+        results = {}
+
         def finish(m, j, on_scalar):
-            result = sb.tile([P, BANK], F32, name=f"result{m}_{j}")
+            group = 1 if j == 2 else 2
+            first = m - m % group
+            if m == first:
+                results[(first, j)] = sb.tile([P, group * BANK], F32, name=f"result{m}_{j}")
+            result = results[(first, j)]
+            dst = result[:, (m - first) * BANK : (m - first + 1) * BANK]
             if on_scalar:
-                nc.scalar.copy(out=result[:], in_=bank_of(m, j)[:])
+                nc.scalar.copy(out=dst, in_=bank_of(m, j)[:])
             else:
-                nc.vector.tensor_copy(out=result[:], in_=bank_of(m, j)[:])
-            nc.sync.dma_start(out=out[m * P : (m + 1) * P, j * BANK : (j + 1) * BANK], in_=result[:])
+                nc.vector.tensor_copy(out=dst, in_=bank_of(m, j)[:])
+            if m == first + group - 1:
+                rows = out[first * P : (first + group) * P, j * BANK : (j + 1) * BANK]
+                nc.sync.dma_start(
+                    out=rows.rearrange("(g p) t -> p g t", p=P),
+                    in_=result[:].rearrange("p (g t) -> p g t", g=group),
+                )
 
         nc.vector.memset(w1_plane[:].bitcast(I32), 0)
         nc.vector.memset(w0_plane[:].bitcast(I32), 0)
@@ -134,29 +139,41 @@ def tile_mix_dconv_fm_none_kernel(tc, x, w0_words, w0_scales, w1_words, w1_scale
         def load_x(c, a):
             return load_rows(f"x_raw{c}_{a}", x, a, X_EDGES[c], X_EDGES[c + 1])
 
+        w1_rows = w1_words.rearrange("a p n i -> a p (n i)")
         x_raw = {(0, 0): load_x(0, 0)}
         load_scales(w1_plane, w1_scales)
-        load_words(w1_codes, w1_words.rearrange("a p n i -> a p (n i)"))
+        load_words(w1_codes, w1_rows, 0)
+        x_raw[(1, 0)] = load_x(1, 0)
+        load_words(w0_codes, w0_words, 0)
         load_scales(w0_plane, w0_scales)
-        load_words(w0_codes, w0_words)
+        x_raw[(2, 0)] = load_x(2, 0)
         x_raw[(0, 1)] = load_x(0, 1)
-        for a in range(PASSES):
-            x_raw[(1, a)] = load_x(1, a)
+        load_words(w1_codes, w1_rows, 1)
+        x_raw[(1, 1)] = load_x(1, 1)
+        load_words(w0_codes, w0_words, 1)
+        x_raw[(2, 1)] = load_x(2, 1)
         w2_raw = [load_rows(f"w2_raw{a}", w2, a, 0, M) for a in range(PASSES)]
-        for c in (2, 3):
+        for c in (3, 4):
             for a in range(PASSES):
                 x_raw[(c, a)] = load_x(c, a)
 
-        def prepare_x(c, a, lead_on_scalar):
-            prepare(f"x_bf{c}_{a}", x_raw[(c, a)], x_codes[a], x_scales[a], X_EDGES[c], lead_on_scalar)
+        def prepare_x(c, a, scalar_helps):
+            prepare(f"x_bf{c}_{a}", x_raw[(c, a)], x_codes[a], x_scales[a], X_EDGES[c], scalar_helps)
 
         ms = range(M_TILES)
-        for j in (0, 1):
-            for a in range(PASSES):
-                prepare_x(j, a, True)
-                for tap in (1, 0):
-                    for m in ms:
-                        multiply(m, j, tap, a)
+        for a in range(PASSES):
+            prepare_x(0, a, True)
+            for m in ms:
+                multiply(m, 0, 1, a, 0, 256)
+            prepare_x(1, a, True)
+            for m in ms:
+                multiply(m, 0, 1, a, 256, 512)
+            for m in ms:
+                multiply(m, 0, 0, a)
+            prepare_x(2, a, True)
+            for tap in (0, 1):
+                for m in ms:
+                    multiply(m, 1, tap, a)
 
         for a in range(PASSES):
             prepare(f"w2_bf{a}", w2_raw[a], w2_codes[a], w2_planes[a], 0, True)
@@ -172,33 +189,34 @@ def tile_mix_dconv_fm_none_kernel(tc, x, w0_words, w0_scales, w1_words, w1_scale
             multiply(m, 2, 1, a, 256, 384)
             multiply(m, 2, 2, a, 0, 256)
 
-        def edge(m):
-            for a in range(PASSES):
-                multiply(m, 2, 1, a, 384, 512)
-                multiply(m, 2, 2, a, 256, 512)
+        def bridge(m):
+            multiply(m, 2, 0, 1)
+            multiply(m, 2, 1, 0, 384, 512)
+            multiply(m, 2, 2, 0, 256, 512)
 
-        finish(0, 0, True)
-        prepare_x(2, 0, True)
-        for m in ms[1:]:
+        def close(m):
+            multiply(m, 2, 1, 1)
+            multiply(m, 2, 2, 1)
+            finish(m, 2, m % 2 == 1)
+
+        prepare_x(3, 0, True)
+        for m in ms:
             finish(m, 0, True)
         for m in ms:
             multiply(m, 1, 2, 0, 384, 512)
-        for m in ms:
+        for m in ms[:2]:
             body(m, 0)
-        prepare_x(2, 1, True)
+        prepare_x(3, 1, False)
         for m in ms:
             multiply(m, 1, 2, 1, 384, 512)
+        body(2, 0)
+        body(3, 0)
         for a in range(PASSES):
-            prepare_x(3, a, False)
+            prepare_x(4, a, False)
         for m in ms:
             finish(m, 1, True)
-        body(0, 1)
-        body(1, 1)
-        edge(0)
-        finish(0, 2, False)
-        edge(1)
-        finish(1, 2, True)
-        for m in (2, 3):
-            body(m, 1)
-            edge(m)
-            finish(m, 2, m == 3)
+        for pair in (ms[:2], ms[2:]):
+            for m in pair:
+                bridge(m)
+            for m in pair:
+                close(m)

@@ -49,16 +49,18 @@ def tile_mix_dconv_fm_none_kernel(tc, x, w0_words, w0_scales, w1_words, w1_scale
             nc.sync.dma_start(out=raw[:], in_=rows.rearrange("(p j) w -> p j w", j=PACK))
             return raw
 
-        def load_scales(plane, scales):
+        def load_scales(queue, plane, scales):
             for q in range(4):
-                nc.sync.dma_start(
+                queue.dma_start(
                     out=plane[32 * q : 32 * q + 4, :].bitcast(I32).rearrange("r (a n) -> r a n", a=PASSES),
                     in_=scales[:, 4 * q : 4 * q + 4, :].bitcast(I32).rearrange("a r n -> r a n"),
                 )
 
-        def load_words(codes, words, a):
-            width = words.shape[2]
-            nc.sync.dma_start(out=codes[:, a * width : (a + 1) * width].bitcast(I32), in_=words[a].bitcast(I32))
+        def load_words(codes, words):
+            nc.sync.dma_start(
+                out=codes[:].bitcast(I32).rearrange("p (a n) -> p a n", a=PASSES),
+                in_=words.bitcast(I32).rearrange("a p n -> p a n"),
+            )
 
         def interleave(name, raw, lo, hi, on_scalar):
             grouped = sb.tile([P, PACK * (hi - lo)], BF16, name=name, align_bytes=ALIGN)
@@ -75,15 +77,10 @@ def tile_mix_dconv_fm_none_kernel(tc, x, w0_words, w0_scales, w1_words, w1_scale
             nc.vector.quantize_mx(out=codes[:, cols].bitcast(FP8X4), scales=plane[:, cols], in_=grouped[:])
 
         def prepare(name, raw, codes, plane, col, scalar_helps):
-            width = raw.shape[2]
-            middle = min(width, LEAD + 256)
-            lead = interleave(name + "_lead", raw, 0, LEAD, scalar_helps)
-            rest = interleave(name + "_rest", raw, LEAD, middle, False)
-            quantise(lead, codes, plane, col)
-            quantise(rest, codes, plane, col + LEAD)
-            if middle < width:
-                tail = interleave(name + "_tail", raw, middle, width, scalar_helps)
-                quantise(tail, codes, plane, col + middle)
+            starts = range(0, raw.shape[2], LEAD)
+            pieces = [interleave(f"{name}_{lo}", raw, lo, lo + LEAD, scalar_helps and lo % (2 * LEAD) > 0) for lo in starts]
+            for lo, grouped in zip(starts, pieces):
+                quantise(grouped, codes, plane, col + lo)
 
         def weight(tap, a, m):
             cols = slice(a * M + m * P, a * M + (m + 1) * P)
@@ -133,24 +130,22 @@ def tile_mix_dconv_fm_none_kernel(tc, x, w0_words, w0_scales, w1_words, w1_scale
                     in_=result[:].rearrange("p (g t) -> p g t", g=group),
                 )
 
-        nc.vector.memset(w1_plane[:].bitcast(I32), 0)
+        nc.gpsimd.memset(w1_plane[:].bitcast(I32), 0)
         nc.vector.memset(w0_plane[:].bitcast(I32), 0)
+        load_scales(nc.gpsimd, w1_plane, w1_scales)
+        load_scales(nc.gpsimd, w0_plane, w0_scales)
 
         def load_x(c, a):
             return load_rows(f"x_raw{c}_{a}", x, a, X_EDGES[c], X_EDGES[c + 1])
 
         w1_rows = w1_words.rearrange("a p n i -> a p (n i)")
         x_raw = {(0, 0): load_x(0, 0)}
-        load_scales(w1_plane, w1_scales)
-        load_words(w1_codes, w1_rows, 0)
+        load_words(w1_codes, w1_rows)
         x_raw[(1, 0)] = load_x(1, 0)
-        load_words(w0_codes, w0_words, 0)
-        load_scales(w0_plane, w0_scales)
+        load_words(w0_codes, w0_words)
         x_raw[(2, 0)] = load_x(2, 0)
         x_raw[(0, 1)] = load_x(0, 1)
-        load_words(w1_codes, w1_rows, 1)
         x_raw[(1, 1)] = load_x(1, 1)
-        load_words(w0_codes, w0_words, 1)
         x_raw[(2, 1)] = load_x(2, 1)
         w2_raw = [load_rows(f"w2_raw{a}", w2, a, 0, M) for a in range(PASSES)]
         for c in (3, 4):
@@ -171,9 +166,13 @@ def tile_mix_dconv_fm_none_kernel(tc, x, w0_words, w0_scales, w1_words, w1_scale
             for m in ms:
                 multiply(m, 0, 0, a)
             prepare_x(2, a, True)
-            for tap in (0, 1):
+            if a == 1:
                 for m in ms:
-                    multiply(m, 1, tap, a)
+                    multiply(m, 1, 1, a, 0, 256)
+            for m in ms:
+                multiply(m, 1, 0, a)
+            for m in ms:
+                multiply(m, 1, 1, a, 256 * a, 512)
 
         for a in range(PASSES):
             prepare(f"w2_bf{a}", w2_raw[a], w2_codes[a], w2_planes[a], 0, True)
@@ -197,7 +196,13 @@ def tile_mix_dconv_fm_none_kernel(tc, x, w0_words, w0_scales, w1_words, w1_scale
         def close(m):
             multiply(m, 2, 1, 1)
             multiply(m, 2, 2, 1)
-            finish(m, 2, m % 2 == 1)
+            if m < M_TILES - 1:
+                finish(m, 2, m % 2 == 1)
+            else:
+                for lo in (0, 256):
+                    half = sb.tile([P, 256], F32, name=f"result_last{lo}")
+                    nc.scalar.copy(out=half[:], in_=bank_of(m, 2)[:, lo : lo + 256])
+                    nc.sync.dma_start(out=out[m * P : (m + 1) * P, 2 * BANK + lo : 2 * BANK + lo + 256], in_=half[:])
 
         prepare_x(3, 0, True)
         for m in ms:
@@ -215,8 +220,10 @@ def tile_mix_dconv_fm_none_kernel(tc, x, w0_words, w0_scales, w1_words, w1_scale
             prepare_x(4, a, False)
         for m in ms:
             finish(m, 1, True)
-        for pair in (ms[:2], ms[2:]):
-            for m in pair:
-                bridge(m)
-            for m in pair:
-                close(m)
+        for m in ms[:2]:
+            bridge(m)
+        for m in ms[:2]:
+            close(m)
+        for m in ms[2:]:
+            bridge(m)
+            close(m)

@@ -130,19 +130,19 @@ def tile_mix_dconv_fm_none_kernel(tc, x, w0_words, w0_scales, w1_words, w1_scale
                     in_=result[:].rearrange("p (g t) -> p g t", g=group),
                 )
 
-        nc.gpsimd.memset(w1_plane[:].bitcast(I32), 0)
+        nc.vector.memset(w1_plane[:].bitcast(I32), 0)
         nc.vector.memset(w0_plane[:].bitcast(I32), 0)
-        load_scales(nc.gpsimd, w1_plane, w1_scales)
-        load_scales(nc.gpsimd, w0_plane, w0_scales)
 
         def load_x(c, a):
             return load_rows(f"x_raw{c}_{a}", x, a, X_EDGES[c], X_EDGES[c + 1])
 
         w1_rows = w1_words.rearrange("a p n i -> a p (n i)")
         x_raw = {(0, 0): load_x(0, 0)}
+        load_scales(nc.sync, w1_plane, w1_scales)
         load_words(w1_codes, w1_rows)
         x_raw[(1, 0)] = load_x(1, 0)
         load_words(w0_codes, w0_words)
+        load_scales(nc.sync, w0_plane, w0_scales)
         x_raw[(2, 0)] = load_x(2, 0)
         x_raw[(0, 1)] = load_x(0, 1)
         x_raw[(1, 1)] = load_x(1, 1)

from contextlib import ExitStack

import concourse.mybir as mybir

D, K, M, T = 128, 1024, 512, 1536
FLOPS = 2 * 3 * K * M * T

F32 = mybir.dt.float32
BF16 = mybir.dt.bfloat16
I32 = mybir.dt.int32
U32 = mybir.dt.uint32
U8 = mybir.dt.uint8
FP8X4 = mybir.dt.float8_e4m3fn_x4
FP4X4 = mybir.dt.float4_e2m1fn_x4

P = 128
PACK = 4
K_PASS = P * PACK
PASSES = K // K_PASS
BANK = 512
M_TILES = M // P
TAPS = 3
X_COLS = T + 2 * D
X_EDGES = (0, 384, 640, 1152, 1536, X_COLS)
LEAD = 128
ALIGN = 256


def tile_mix_dconv_fm_none_kernel(tc, x, w0_words, w0_scales, w1_words, w1_scales, w2, out):
    nc = tc.nc
    with ExitStack() as ctx:
        sb = ctx.enter_context(tc.tile_pool(name="sb", bufs=1))
        psum = ctx.enter_context(tc.psum_pool(name="psum", bufs=1))
        ctx.enter_context(tc.manual_schedule())

        x_codes = [sb.tile([P, X_COLS], U32, name=f"x_codes{a}", align_bytes=ALIGN) for a in range(PASSES)]
        x_scales = [sb.tile([P, X_COLS], U8, name=f"x_scales{a}", align_bytes=ALIGN) for a in range(PASSES)]
        w2_codes = [sb.tile([P, M], U32, name=f"w2_codes{a}", align_bytes=ALIGN) for a in range(PASSES)]
        w2_planes = [sb.tile([P, M], U8, name=f"w2_scales{a}", align_bytes=ALIGN) for a in range(PASSES)]
        w0_codes = sb.tile([P, PASSES * 2 * M], U8, name="w0_codes", align_bytes=ALIGN)
        w1_codes = sb.tile([P, PASSES * 4 * M], U8, name="w1_codes", align_bytes=ALIGN)
        w0_plane = sb.tile([P, PASSES * M], U8, name="w0_plane", align_bytes=ALIGN)
        w1_plane = sb.tile([P, PASSES * M], U8, name="w1_plane", align_bytes=ALIGN)
        banks = [psum.tile([P, BANK], F32, name=f"bank{b}") for b in range(2 * M_TILES)]

        def load_rows(name, src, a, lo, hi):
            raw = sb.tile([P, PACK, hi - lo], F32, name=name)
            rows = src[a * K_PASS : (a + 1) * K_PASS, lo:hi]
            nc.sync.dma_start(out=raw[:], in_=rows.rearrange("(p j) w -> p j w", j=PACK))
            return raw

        def load_scales(queue, plane, scales):
            for q in range(4):
                queue.dma_start(
                    out=plane[32 * q : 32 * q + 4, :].bitcast(I32).rearrange("r (a n) -> r a n", a=PASSES),
                    in_=scales[:, 4 * q : 4 * q + 4, :].bitcast(I32).rearrange("a r n -> r a n"),
                )

        def load_words(codes, words):
            nc.sync.dma_start(
                out=codes[:].bitcast(I32).rearrange("p (a n) -> p a n", a=PASSES),
                in_=words.bitcast(I32).rearrange("a p n -> p a n"),
            )

        def interleave(name, raw, lo, hi, on_scalar):
            grouped = sb.tile([P, PACK * (hi - lo)], BF16, name=name, align_bytes=ALIGN)
            dst = grouped[:].rearrange("p (c i t) -> p c t i", i=4, t=PACK)
            src = raw[:, :, lo:hi].rearrange("p t (c i) -> p c t i", i=4)
            if on_scalar:
                nc.scalar.copy(out=dst, in_=src)
            else:
                nc.vector.tensor_copy(out=dst, in_=src)
            return grouped

        def quantise(grouped, codes, plane, col):
            cols = slice(col, col + grouped.shape[1] // PACK)
            nc.vector.quantize_mx(out=codes[:, cols].bitcast(FP8X4), scales=plane[:, cols], in_=grouped[:])

        def prepare(name, raw, codes, plane, col, scalar_helps):
            starts = range(0, raw.shape[2], LEAD)
            pieces = [interleave(f"{name}_{lo}", raw, lo, lo + LEAD, scalar_helps and lo % (2 * LEAD) > 0) for lo in starts]
            for lo, grouped in zip(starts, pieces):
                quantise(grouped, codes, plane, col + lo)

        def weight(tap, a, m):
            cols = slice(a * M + m * P, a * M + (m + 1) * P)
            if tap == 0:
                return w0_codes[:, 2 * cols.start : 2 * cols.stop].bitcast(FP4X4), w0_plane[:, cols]
            if tap == 1:
                return w1_codes[:, 4 * cols.start : 4 * cols.stop].bitcast(FP8X4), w1_plane[:, cols]
            return w2_codes[a][:, m * P : (m + 1) * P].bitcast(FP8X4), w2_planes[a][:, m * P : (m + 1) * P]

        summed = {}

        def bank_of(m, j):
            return banks[(j % 2) * M_TILES + m]

        def multiply(m, j, tap, a, lo=0, hi=BANK):
            before = summed.get((m, j), 0)
            summed[(m, j)] = before + hi - lo
            codes, plane = weight(tap, a, m)
            cols = slice(j * BANK + tap * D + lo, j * BANK + tap * D + hi)
            nc.tensor.matmul_mx(
                out=bank_of(m, j)[:, lo:hi],
                lhsT=codes,
                lhsT_scale=plane,
                rhs=x_codes[a][:, cols].bitcast(FP8X4),
                rhs_scale=x_scales[a][:, cols],
                start=(before == 0),
                stop=(summed[(m, j)] == TAPS * PASSES * BANK),
            )

        results = {}

        def finish(m, j, on_scalar):
            group = 1 if j == 2 else 2
            first = m - m % group
            if m == first:
                results[(first, j)] = sb.tile([P, group * BANK], F32, name=f"result{m}_{j}")
            result = results[(first, j)]
            dst = result[:, (m - first) * BANK : (m - first + 1) * BANK]
            if on_scalar:
                nc.scalar.copy(out=dst, in_=bank_of(m, j)[:])
            else:
                nc.vector.tensor_copy(out=dst, in_=bank_of(m, j)[:])
            if m == first + group - 1:
                rows = out[first * P : (first + group) * P, j * BANK : (j + 1) * BANK]
                nc.sync.dma_start(
                    out=rows.rearrange("(g p) t -> p g t", p=P),
                    in_=result[:].rearrange("p (g t) -> p g t", g=group),
                )

        nc.vector.memset(w1_plane[:].bitcast(I32), 0)
        nc.vector.memset(w0_plane[:].bitcast(I32), 0)

        def load_x(c, a):
            return load_rows(f"x_raw{c}_{a}", x, a, X_EDGES[c], X_EDGES[c + 1])

        w1_rows = w1_words.rearrange("a p n i -> a p (n i)")
        x_raw = {(0, 0): load_x(0, 0)}
        load_scales(nc.sync, w1_plane, w1_scales)
        load_words(w1_codes, w1_rows)
        x_raw[(1, 0)] = load_x(1, 0)
        load_words(w0_codes, w0_words)
        load_scales(nc.sync, w0_plane, w0_scales)
        x_raw[(2, 0)] = load_x(2, 0)
        x_raw[(0, 1)] = load_x(0, 1)
        x_raw[(1, 1)] = load_x(1, 1)
        x_raw[(2, 1)] = load_x(2, 1)
        w2_raw = [load_rows(f"w2_raw{a}", w2, a, 0, M) for a in range(PASSES)]
        for c in (3, 4):
            for a in range(PASSES):
                x_raw[(c, a)] = load_x(c, a)

        def prepare_x(c, a, scalar_helps):
            prepare(f"x_bf{c}_{a}", x_raw[(c, a)], x_codes[a], x_scales[a], X_EDGES[c], scalar_helps)

        ms = range(M_TILES)
        for a in range(PASSES):
            prepare_x(0, a, True)
            for m in ms:
                multiply(m, 0, 1, a, 0, 256)
            prepare_x(1, a, True)
            for m in ms:
                multiply(m, 0, 1, a, 256, 512)
            for m in ms:
                multiply(m, 0, 0, a)
            prepare_x(2, a, True)
            if a == 1:
                for m in ms:
                    multiply(m, 1, 1, a, 0, 256)
            for m in ms:
                multiply(m, 1, 0, a)
            for m in ms:
                multiply(m, 1, 1, a, 256 * a, 512)

        for a in range(PASSES):
            prepare(f"w2_bf{a}", w2_raw[a], w2_codes[a], w2_planes[a], 0, True)
            for m in ms:
                multiply(m, 0, 2, a)
            for m in ms:
                multiply(m, 1, 2, a, 0, 256)
                multiply(m, 1, 2, a, 256, 384)

        def body(m, a):
            multiply(m, 2, 0, a)
            multiply(m, 2, 1, a, 0, 256)
            multiply(m, 2, 1, a, 256, 384)
            multiply(m, 2, 2, a, 0, 256)

        def bridge(m):
            multiply(m, 2, 0, 1)
            multiply(m, 2, 1, 0, 384, 512)
            multiply(m, 2, 2, 0, 256, 512)

        def close(m):
            multiply(m, 2, 1, 1)
            multiply(m, 2, 2, 1)
            if m < M_TILES - 1:
                finish(m, 2, m % 2 == 1)
            else:
                for lo in (0, 256):
                    half = sb.tile([P, 256], F32, name=f"result_last{lo}")
                    nc.scalar.copy(out=half[:], in_=bank_of(m, 2)[:, lo : lo + 256])
                    nc.sync.dma_start(out=out[m * P : (m + 1) * P, 2 * BANK + lo : 2 * BANK + lo + 256], in_=half[:])

        prepare_x(3, 0, True)
        for m in ms:
            finish(m, 0, True)
        for m in ms:
            multiply(m, 1, 2, 0, 384, 512)
        for m in ms[:2]:
            body(m, 0)
        prepare_x(3, 1, False)
        for m in ms:
            multiply(m, 1, 2, 1, 384, 512)
        body(2, 0)
        body(3, 0)
        for a in range(PASSES):
            prepare_x(4, a, False)
        for m in ms:
            finish(m, 1, True)
        for m in ms[:2]:
            bridge(m)
        for m in ms[:2]:
            close(m)
        for m in ms[2:]:
            bridge(m)
            close(m)
